import numpy as np
import ml_dtypes


def mxq(x, axis, fmt="e4m3"):
    dtype, down = {"e4m3": (ml_dtypes.float8_e4m3fn, 7), "e5m2": (ml_dtypes.float8_e5m2, 14)}[fmt]
    v = np.moveaxis(np.asarray(x, np.float32).astype(ml_dtypes.bfloat16).astype(np.float64), axis, -1)
    blocks = v.reshape(v.shape[:-1] + (-1, 32))
    amax = np.abs(blocks).max(-1, keepdims=True)
    byte = np.maximum(np.where(amax > 0, np.frexp(amax)[1] - 1 + 127, 0) - down, 1)
    scale = np.exp2(byte - 127.0)
    codes = (blocks / scale).astype(np.float32).astype(dtype).astype(np.float64)
    return np.moveaxis((codes * scale).reshape(v.shape), -1, axis)


WIDE = False


def mx_kscale(k):
    if not WIDE:
        return np.ones(k)
    levels = np.array([18, -18])
    if k % 512:
        return np.exp2(np.random.permutation(np.resize(levels, k // 32))).repeat(32)
    a = np.empty((k // 512, 16))
    for p in range(k // 512):
        a[p, :8] = np.random.permutation(np.resize(levels, 8))
        for g in range(8):
            far = levels[np.abs(levels - a[p, g]) >= 10]
            a[p, g + 8] = far[np.random.randint(len(far))]
    return np.exp2(a.ravel()).repeat(32)


def f64(x):
    return np.asarray(x).astype(np.float64)


def striped(idx):
    return np.tile(np.asarray(idx).reshape(-1, 16).T, (8, 1)).astype(np.uint16)


def unstriped(offs):
    return offs[:16].T.reshape(-1).astype(np.int64)


E2M1 = np.array([0.0, 0.5, 1.0, 1.5, 2.0, 3.0, 4.0, 6.0, -0.0, -0.5, -1.0, -1.5, -2.0, -3.0, -4.0, -6.0])


def pack_weight(w, fmt):
    k, n = w.shape
    w = f64(np.asarray(w, np.float32).astype(ml_dtypes.bfloat16)).reshape(k // 32, 32, n)
    amax = np.abs(w).max(1)
    if fmt == "e4m3":
        byte = np.frexp(amax)[1] - 1 + 127 - 7
    else:
        mant, ex = np.frexp(amax / 6.0)
        byte = np.where(mant > 0.5, ex, ex - 1) + 127
    byte = np.clip(np.where(amax > 0, byte, 1), 1, 254)
    scaled = (w * np.exp2(127.0 - byte)[:, None, :]).reshape(k, n).astype(np.float32)
    by_word = np.ascontiguousarray(scaled.reshape(k // 512, 128, 4, n).transpose(0, 1, 3, 2))
    if fmt == "e4m3":
        words = by_word.astype(ml_dtypes.float8_e4m3fn).view(np.uint8)
    else:
        c = by_word.astype(ml_dtypes.float4_e2m1fn).view(np.uint8) & 0xF
        words = (c[..., 0::2] | (c[..., 1::2] << 4)).reshape(k // 512, 128, 2 * n)
    return np.ascontiguousarray(words), np.ascontiguousarray(byte.astype(np.uint8).reshape(k // 512, 16, n))


def unpack_weight(words, scales, fmt):
    g, _, n = scales.shape
    words = np.ascontiguousarray(words).reshape(g, 128, n, -1)
    if fmt == "e4m3":
        vals = words.view(ml_dtypes.float8_e4m3fn).astype(np.float64)
    else:
        nib = np.empty((g, 128, n, 4), np.uint8)
        nib[..., 0::2] = words & 0xF
        nib[..., 1::2] = words >> 4
        vals = E2M1[nib]
    vals = vals * np.repeat(np.exp2(scales.astype(np.float64) - 127.0), 8, axis=1)[..., None]
    return vals.transpose(0, 1, 3, 2).reshape(g * 512, n)


N, T, D, V = 512, 1024, 512, 1024


def setup_inputs():
    n = np.random.standard_normal
    idx = np.random.permutation(T)[:N]
    s = mx_kscale(D)[:, None]
    z = mx_kscale(V)[:, None]
    w = n((D, V)) / np.sqrt(D)
    wd, wv = pack_weight(w * s, "e2m1"), pack_weight(w.T / z, "e2m1")
    return {
        "xT": (n((D, T)) / s).astype(np.float32),
        "wd_words": wd[0],
        "wd_scales": wd[1],
        "wv_words": wv[0],
        "wv_scales": wv[1],
        "y": (2 * np.random.randint(0, 2, (V, N)) - 1).astype(np.float32),
        "cw": (np.random.uniform(0.5, 1.5, (V, 1)) / np.sqrt(V) * z).astype(np.float32),
        "rw": np.tile(np.random.uniform(0.5, 1.5, N), (128, 1)).astype(np.float32),
        "offs": striped(idx),
    }


def reference(xT, wd_words, wd_scales, wv_words, wv_scales, y, cw, rw, offs):
    idx = unstriped(offs)
    a = unpack_weight(wd_words, wd_scales, "e2m1").T @ mxq(f64(xT)[:, idx], 0, "e4m3")
    g = -f64(cw) * f64(rw)[:1] * f64(y) / (1.0 + np.exp(f64(y) * a))
    dx = unpack_weight(wv_words, wv_scales, "e2m1").T @ mxq(g, 0, "e5m2")
    gx = np.zeros((D, T))
    gx[:, idx] = dx
    return gx

@@ -1,0 +1,243 @@
+from contextlib import ExitStack
+
+import concourse.mybir as mybir
+from concourse.masks import make_identity
+
+N, T, D, V = 512, 1024, 512, 1024
+FLOPS = 2 * 2 * N * D * V
+
+F32 = mybir.dt.float32
+BF16 = mybir.dt.bfloat16
+I32 = mybir.dt.int32
+U32 = mybir.dt.uint32
+U16 = mybir.dt.uint16
+U8 = mybir.dt.uint8
+E4M3 = mybir.dt.float8_e4m3fn_x4
+E5M2 = mybir.dt.float8_e5m2_x4
+E2M1 = mybir.dt.float4_e2m1fn_x4
+MULT = mybir.AluOpType.mult
+SIGMOID = mybir.ActivationFunctionType.Sigmoid
+COPY = mybir.ActivationFunctionType.Copy
+
+P = 128
+LANES = 4
+PASS = P * LANES
+HALF = N // 2
+PASSES = V // PASS
+EARLY = 1
+
+
+def tile_attend_gml_sig_kernel(tc, xT, wd_words, wd_scales, wv_words, wv_scales, y, cw, rw, offs, out):
+    nc = tc.nc
+    with ExitStack() as ctx:
+        keep = ctx.enter_context(tc.tile_pool(name="keep", bufs=1))
+        ring = ctx.enter_context(tc.tile_pool(name="ring", bufs=2))
+        score_psum = ctx.enter_context(tc.psum_pool(name="score_psum", bufs=4))
+        grad_psum = ctx.enter_context(tc.psum_pool(name="grad_psum", bufs=1))
+
+        offsets = keep.tile([P, N // 16], U16, name="offsets")
+        nc.sync.dma_start(offsets[:], offs)
+
+        def listed(h):
+            return offsets[:, h * HALF // 16 : (h + 1) * HALF // 16]
+
+        wd_scale_raw = keep.tile([P, V], U8, name="wd_scale_raw", align_bytes=64)
+        wv_scale = keep.tile([P, PASSES, D], U8, name="wv_scale", align_bytes=64)
+        nc.vector.memset(wd_scale_raw[:].bitcast(I32), 0)
+        nc.vector.memset(wv_scale[:].rearrange("p o d -> p (o d)").bitcast(I32), 0)
+
+        identity = keep.tile([P, P], F32, name="identity")
+        make_identity(nc, identity[:])
+
+        rw_cols = keep.tile([P, LANES], F32, name="rw_cols")
+        nc.scalar.dma_start(rw_cols[:], rw[0:1, :].rearrange("one (p j) -> (one p) j", j=LANES))
+        cw_cols = keep.tile([P, PASSES, LANES], F32, name="cw_cols")
+        nc.scalar.dma_start(cw_cols[:], cw.rearrange("(o p t) one -> p o (t one)", o=PASSES, t=LANES))
+        for q in range(4):
+            nc.scalar.dma_start(
+                wd_scale_raw[32 * q : 32 * q + 4, :].bitcast(I32),
+                wd_scales[0, 4 * q : 4 * q + 4, :].bitcast(I32),
+            )
+        warm = keep.tile([P, 8], F32, name="warm")
+        nc.scalar.activation(warm[:], identity[:, 0:8], SIGMOID)
+
+        x_rows = xT.rearrange("(p t) n -> t p n", t=LANES)
+        planes = []
+        for t in range(LANES):
+            plane = keep.tile([P, T], F32, name=f"plane{t}")
+            nc.sync.dma_start(plane[:], x_rows[t])
+            planes.append(plane)
+        wd_raw = keep.tile([P, 2 * V], U8, name="wd_raw", align_bytes=64)
+        nc.sync.dma_start(wd_raw[:].bitcast(I32), wd_words[0].bitcast(I32))
+        y_rows = y.rearrange("(o p t) n -> o p t n", o=PASSES, t=LANES)
+        labels = {}
+        wv_codes = keep.tile([P, PASSES, 2 * D], U8, name="wv_codes", align_bytes=64)
+        for h in range(2):
+            for o in range(PASSES):
+                labels[o, h] = keep.tile([P, LANES, HALF], F32, name=f"labels{o}{h}")
+                nc.sync.dma_start(labels[o, h][:], y_rows[o, :, :, h * HALF : (h + 1) * HALF])
+            if h == 0:
+                nc.sync.dma_start(
+                    wv_codes[:].rearrange("p o n -> p (o n)").bitcast(I32).rearrange("p (o n) -> p o n", o=PASSES),
+                    wv_words.bitcast(I32).rearrange("o p n -> p o n"),
+                )
+        for q in range(4):
+            nc.sync.dma_start(
+                wv_scale[32 * q : 32 * q + 4, :, :].rearrange("p o d -> p (o d)").bitcast(I32).rearrange("p (o d) -> p o d", o=PASSES),
+                wv_scales.bitcast(I32)[:, 4 * q : 4 * q + 4, :].rearrange("o f d -> f o d"),
+            )
+
+        g_codes = [keep.tile([P, N], U32, name=f"g_codes{o}", align_bytes=64) for o in range(PASSES)]
+        g_scale = [keep.tile([P, N], U8, name=f"g_scale{o}", align_bytes=64) for o in range(PASSES)]
+        for o in range(PASSES):
+            nc.vector.memset(g_codes[o][:, HALF:].bitcast(I32), 0)
+            nc.vector.memset(g_scale[o][:, HALF:].bitcast(I32), 0)
+
+        windows = []
+        for j in range(D // P):
+            window = keep.tile([P, T], F32, name=f"window{j}")
+            (nc.vector if j < 2 else nc.gpsimd).memset(window[:], 0.0)
+            windows.append(window)
+
+        neg_cw = keep.tile([P, PASSES, LANES], F32, name="neg_cw")
+        nc.scalar.mul(neg_cw[:], cw_cols[:], -1.0)
+        rw_bank = score_psum.tile([P, LANES, P], F32, name="bank")
+        for j in range(LANES):
+            nc.tensor.transpose(rw_bank[:, j, :], rw_cols[:, j : j + 1].to_broadcast([P, P]), identity[:])
+        factor = [keep.tile([P, LANES, N], F32, name=f"factor{o}") for o in range(PASSES)]
+        for o in range(PASSES):
+            for r in range(LANES):
+                nc.scalar.activation(
+                    factor[o][:, r, :].rearrange("p (k j) -> p k j", j=LANES),
+                    rw_bank[:].rearrange("p j k -> p k j"),
+                    COPY,
+                    scale=neg_cw[:, o, r : r + 1],
+                )
+
+        wd_scale = keep.tile([P, V], U8, name="wd_scale", align_bytes=64)
+        nc.vector.tensor_copy(
+            wd_scale[:].rearrange("p (o r s) -> p o r s", o=PASSES, r=LANES),
+            wd_scale_raw[:].rearrange("p (o s r) -> p o r s", o=PASSES, r=LANES),
+        )
+
+        gathered = keep.tile([P, LANES, N], BF16, name="gathered")
+        for t in range(LANES - 1):
+            nc.vector.tensor_copy(gathered[:, t, :], planes[t][:].indirect(offsets[:]))
+
+        wd_codes, x_codes, x_scale = [], [], []
+        for h in range(2):
+            cols = slice(h * HALF, (h + 1) * HALF)
+            nc.vector.tensor_copy(gathered[:, LANES - 1, cols], planes[LANES - 1][:].indirect(listed(h)))
+            woven = keep.tile([P, HALF, LANES], BF16, name=f"woven{h}", tag=f"woven{h}", align_bytes=64)
+            nc.vector.tensor_copy(
+                woven[:].rearrange("p (c i) t -> p c t i", i=4),
+                gathered[:, :, cols].rearrange("p t (c i) -> p c t i", i=4),
+            )
+            dealt = keep.tile([P, 2 * PASS], U8, name=f"wd_codes{h}", align_bytes=64)
+            nc.vector.tensor_copy(
+                dealt[:].bitcast(U16).rearrange("p (r s) -> p r s", r=LANES),
+                wd_raw[:].bitcast(U16)[:, h * PASS : (h + 1) * PASS].rearrange("p (s r) -> p r s", r=LANES),
+            )
+            wd_codes.append(dealt)
+            codes = keep.tile([P, HALF], U32, name=f"x_codes{h}", align_bytes=64)
+            scale = keep.tile([P, HALF], U8, name=f"x_scale{h}", align_bytes=64)
+            nc.vector.quantize_mx(codes[:].bitcast(E4M3), scale[:], woven[:].rearrange("p i t -> p (i t)"))
+            x_codes.append(codes)
+            x_scale.append(scale)
+
+        sig, weighted, g_in, dx = {}, {}, {}, {}
+
+        def scores(o, h):
+            sig[o, h] = ring.tile([P, LANES, HALF], F32, name="sig")
+            for pair in range(2):
+                bank = score_psum.tile([P, 2, HALF], F32, name="bank")
+                for e in range(2):
+                    r = 2 * pair + e
+                    nc.tensor.matmul_mx(
+                        bank[:, e, :],
+                        lhsT=wd_codes[o][:, 2 * P * r : 2 * P * (r + 1)].bitcast(E2M1),
+                        lhsT_scale=wd_scale[:, o * PASS + P * r : o * PASS + P * (r + 1)],
+                        rhs=x_codes[h][:].bitcast(E4M3),
+                        rhs_scale=x_scale[h][:],
+                        start=True,
+                        stop=True,
+                    )
+                margin = ring.tile([P, 2, HALF], F32, name="margin", bufs=4)
+                nc.vector.tensor_tensor(margin[:], bank[:], labels[o, h][:, 2 * pair : 2 * pair + 2, :], MULT)
+                nc.scalar.activation(sig[o, h][:, 2 * pair : 2 * pair + 2, :], margin[:], SIGMOID, scale=-1.0)
+
+        def weigh(o, h, engine, tag):
+            weighted[o, h] = keep.tile([P, LANES, HALF], F32, name=f"weighted{o}{h}", tag=tag, align_bytes=64)
+            engine.tensor_tensor(weighted[o, h][:], labels[o, h][:], factor[o][:, :, h * HALF : (h + 1) * HALF], MULT)
+
+        def gradient(o, h, first, count):
+            if first == 0:
+                g_in[o, h] = keep.tile([P, HALF, LANES], BF16, name=f"g_in{o}{h}", tag=f"g_in{o}{h}", align_bytes=64)
+            cols = slice(first, first + count)
+            nc.vector.tensor_tensor(
+                g_in[o, h][:, cols, :].rearrange("p (c i) t -> p c t i", i=2),
+                sig[o, h][:, :, cols].rearrange("p t (c i) -> p c t i", i=2),
+                weighted[o, h][:, :, cols].rearrange("p t (c i) -> p c t i", i=2),
+                MULT,
+            )
+
+        def quantise(o, h, first, count):
+            cols = slice(h * HALF + first, h * HALF + first + count)
+            nc.vector.quantize_mx(
+                g_codes[o][:, cols].bitcast(E5M2),
+                g_scale[o][:, cols],
+                g_in[o, h][:, first : first + count, :].rearrange("p i t -> p (i t)"),
+            )
+
+        def back(bank, o, j):
+            nc.tensor.matmul_mx(
+                bank[:],
+                lhsT=wv_codes[:, o, 2 * P * j : 2 * P * (j + 1)].bitcast(E2M1),
+                lhsT_scale=wv_scale[:, o, P * j : P * (j + 1)],
+                rhs=g_codes[o][:].bitcast(E5M2),
+                rhs_scale=g_scale[o][:],
+                start=(o == 0),
+                stop=(o == PASSES - 1),
+            )
+
+        scores(0, 0)
+        weigh(0, 0, nc.vector, "w00")
+        scores(1, 0)
+        gradient(0, 0, 0, HALF)
+        weigh(1, 0, nc.vector, "w10")
+        quantise(0, 0, 0, HALF)
+        gradient(1, 0, 0, HALF)
+        scores(0, 1)
+        quantise(1, 0, 0, HALF)
+        for j in range(EARLY):
+            bank = grad_psum.tile([P, N], F32, name=f"grad{j}")
+            for o in range(PASSES):
+                back(bank, o, j)
+            dx[j, 0] = keep.tile([P, HALF], F32, name=f"dx_early{j}")
+            nc.scalar.copy(dx[j, 0][:], bank[:, :HALF])
+        weigh(0, 1, nc.vector, "w01")
+        scores(1, 1)
+        gradient(0, 1, 0, HALF)
+        weigh(1, 1, nc.vector, "w11")
+        quantise(0, 1, 0, HALF)
+        grad = [grad_psum.tile([P, N], F32, name=f"grad{j}") for j in range(D // P)]
+        for j in range(D // P):
+            back(grad[j], 0, j)
+        gradient(1, 1, 0, HALF // 2)
+        gradient(1, 1, HALF // 2, HALF // 2)
+        quantise(1, 1, 0, HALF // 2)
+        quantise(1, 1, HALF // 2, HALF // 2)
+        for j in range(D // P):
+            back(grad[j], 1, j)
+        for j in range(EARLY):
+            nc.vector.tensor_copy(windows[j][:].indirect(listed(0)), dx[j, 0][:])
+        for j in range(D // P):
+            if j < EARLY:
+                dx[j, 1] = keep.tile([P, HALF], F32, name=f"dx{j}")
+                nc.scalar.copy(dx[j, 1][:], grad[j][:, HALF:])
+                nc.vector.tensor_copy(windows[j][:].indirect(listed(1)), dx[j, 1][:])
+            else:
+                dx[j, 1] = keep.tile([P, N], F32, name=f"dx{j}")
+                nc.scalar.copy(dx[j, 1][:], grad[j][:])
+                nc.vector.tensor_copy(windows[j][:].indirect(offsets[:]), dx[j, 1][:])
+            nc.sync.dma_start(out[P * j : P * (j + 1), :], windows[j][:])

@@ -22,9 +22,11 @@ COPY = mybir.ActivationFunctionType.Copy
 P = 128
 LANES = 4
 PASS = P * LANES
-HALF = N // 2
 PASSES = V // PASS
-EARLY = 1
+HALF = N // 2
+QUADRANTS = 4
+OUT_TILES = D // P
+PAIR = 2
 
 
 def tile_attend_gml_sig_kernel(tc, xT, wd_words, wd_scales, wv_words, wv_scales, y, cw, rw, offs, out):
@@ -32,56 +34,55 @@ def tile_attend_gml_sig_kernel(tc, xT, wd_words, wd_scales, wv_words, wv_scales,
     with ExitStack() as ctx:
         keep = ctx.enter_context(tc.tile_pool(name="keep", bufs=1))
         ring = ctx.enter_context(tc.tile_pool(name="ring", bufs=2))
-        score_psum = ctx.enter_context(tc.psum_pool(name="score_psum", bufs=4))
-        grad_psum = ctx.enter_context(tc.psum_pool(name="grad_psum", bufs=1))
+        psum = ctx.enter_context(tc.psum_pool(name="psum", bufs=1))
 
         offsets = keep.tile([P, N // 16], U16, name="offsets")
-        nc.sync.dma_start(offsets[:], offs)
 
         def listed(h):
             return offsets[:, h * HALF // 16 : (h + 1) * HALF // 16]
 
         wd_scale_raw = keep.tile([P, V], U8, name="wd_scale_raw", align_bytes=64)
         wv_scale = keep.tile([P, PASSES, D], U8, name="wv_scale", align_bytes=64)
-        nc.vector.memset(wd_scale_raw[:].bitcast(I32), 0)
-        nc.vector.memset(wv_scale[:].rearrange("p o d -> p (o d)").bitcast(I32), 0)
-
+        nc.gpsimd.memset(wd_scale_raw[:].bitcast(I32), 0)
         identity = keep.tile([P, P], F32, name="identity")
         make_identity(nc, identity[:])
+        nc.vector.memset(wv_scale[:].rearrange("p o d -> p (o d)").bitcast(I32), 0)
 
         rw_cols = keep.tile([P, LANES], F32, name="rw_cols")
-        nc.scalar.dma_start(rw_cols[:], rw[0:1, :].rearrange("one (p j) -> (one p) j", j=LANES))
+        nc.sync.dma_start(rw_cols[:], rw[0:1, :].rearrange("one (p j) -> (one p) j", j=LANES))
         cw_cols = keep.tile([P, PASSES, LANES], F32, name="cw_cols")
-        nc.scalar.dma_start(cw_cols[:], cw.rearrange("(o p t) one -> p o (t one)", o=PASSES, t=LANES))
-        for q in range(4):
-            nc.scalar.dma_start(
+        nc.scalar.dma_start(cw_cols[:], cw.rearrange("(o p r) one -> p o (r one)", o=PASSES, r=LANES))
+
+        x_rows = xT.rearrange("(p r) n -> r p n", r=LANES)
+        planes = [keep.tile([P, T], F32, name=f"plane{r}") for r in range(LANES)]
+        nc.sync.dma_start(planes[0][:], x_rows[0])
+        nc.sync.dma_start(offsets[:], offs)
+        for r in range(1, LANES):
+            nc.sync.dma_start(planes[r][:], x_rows[r])
+        for q in range(QUADRANTS):
+            nc.sync.dma_start(
                 wd_scale_raw[32 * q : 32 * q + 4, :].bitcast(I32),
                 wd_scales[0, 4 * q : 4 * q + 4, :].bitcast(I32),
             )
-        warm = keep.tile([P, 8], F32, name="warm")
-        nc.scalar.activation(warm[:], identity[:, 0:8], SIGMOID)
-
-        x_rows = xT.rearrange("(p t) n -> t p n", t=LANES)
-        planes = []
-        for t in range(LANES):
-            plane = keep.tile([P, T], F32, name=f"plane{t}")
-            nc.sync.dma_start(plane[:], x_rows[t])
-            planes.append(plane)
         wd_raw = keep.tile([P, 2 * V], U8, name="wd_raw", align_bytes=64)
         nc.sync.dma_start(wd_raw[:].bitcast(I32), wd_words[0].bitcast(I32))
-        y_rows = y.rearrange("(o p t) n -> o p t n", o=PASSES, t=LANES)
+
+        y_rows = y.rearrange("(o p r) n -> o p r n", o=PASSES, r=LANES)
         labels = {}
-        wv_codes = keep.tile([P, PASSES, 2 * D], U8, name="wv_codes", align_bytes=64)
-        for h in range(2):
+
+        def load_labels(h):
             for o in range(PASSES):
                 labels[o, h] = keep.tile([P, LANES, HALF], F32, name=f"labels{o}{h}")
                 nc.sync.dma_start(labels[o, h][:], y_rows[o, :, :, h * HALF : (h + 1) * HALF])
-            if h == 0:
-                nc.sync.dma_start(
-                    wv_codes[:].rearrange("p o n -> p (o n)").bitcast(I32).rearrange("p (o n) -> p o n", o=PASSES),
-                    wv_words.bitcast(I32).rearrange("o p n -> p o n"),
-                )
-        for q in range(4):
+
+        load_labels(0)
+        wv_codes = keep.tile([P, PASSES, 2 * D], U8, name="wv_codes", align_bytes=64)
+        nc.sync.dma_start(
+            wv_codes[:].rearrange("p o n -> p (o n)").bitcast(I32).rearrange("p (o n) -> p o n", o=PASSES),
+            wv_words.bitcast(I32).rearrange("o p n -> p o n"),
+        )
+        load_labels(1)
+        for q in range(QUADRANTS):
             nc.sync.dma_start(
                 wv_scale[32 * q : 32 * q + 4, :, :].rearrange("p o d -> p (o d)").bitcast(I32).rearrange("p (o d) -> p o d", o=PASSES),
                 wv_scales.bitcast(I32)[:, 4 * q : 4 * q + 4, :].rearrange("o f d -> f o d"),
@@ -94,150 +95,148 @@ def tile_attend_gml_sig_kernel(tc, xT, wd_words, wd_scales, wv_words, wv_scales,
             nc.vector.memset(g_scale[o][:, HALF:].bitcast(I32), 0)
 
         windows = []
-        for j in range(D // P):
+        for j in range(OUT_TILES):
             window = keep.tile([P, T], F32, name=f"window{j}")
-            (nc.vector if j < 2 else nc.gpsimd).memset(window[:], 0.0)
+            (nc.vector if j < OUT_TILES // 2 else nc.gpsimd).memset(window[:].bitcast(I32), 0)
             windows.append(window)
 
-        neg_cw = keep.tile([P, PASSES, LANES], F32, name="neg_cw")
-        nc.scalar.mul(neg_cw[:], cw_cols[:], -1.0)
-        rw_bank = score_psum.tile([P, LANES, P], F32, name="bank")
+        neg_cw = []
+        for o, tag in enumerate(("second_half_gate", "neg_cw1")):
+            neg_cw.append(keep.tile([P, LANES], F32, name=f"neg_cw{o}", tag=tag, align_bytes=64))
+            nc.scalar.mul(neg_cw[o][:], cw_cols[:, o, :], -1.0)
+
+        rw_bank = psum.tile([P, LANES, P], F32, name="rw_bank")
         for j in range(LANES):
             nc.tensor.transpose(rw_bank[:, j, :], rw_cols[:, j : j + 1].to_broadcast([P, P]), identity[:])
-        factor = [keep.tile([P, LANES, N], F32, name=f"factor{o}") for o in range(PASSES)]
-        for o in range(PASSES):
-            for r in range(LANES):
-                nc.scalar.activation(
-                    factor[o][:, r, :].rearrange("p (k j) -> p k j", j=LANES),
-                    rw_bank[:].rearrange("p j k -> p k j"),
-                    COPY,
-                    scale=neg_cw[:, o, r : r + 1],
-                )
+        rw_row = rw_bank[:].rearrange("p j k -> p k j")
 
-        wd_scale = keep.tile([P, V], U8, name="wd_scale", align_bytes=64)
-        nc.vector.tensor_copy(
-            wd_scale[:].rearrange("p (o r s) -> p o r s", o=PASSES, r=LANES),
-            wd_scale_raw[:].rearrange("p (o s r) -> p o r s", o=PASSES, r=LANES),
-        )
+        factor = keep.tile([P, LANES, N], F32, name="factor")
+        for r in range(LANES):
+            nc.scalar.activation(
+                factor[:, r, :].rearrange("p (k j) -> p k j", j=LANES), rw_row, COPY, scale=neg_cw[0][:, r : r + 1]
+            )
 
         gathered = keep.tile([P, LANES, N], BF16, name="gathered")
-        for t in range(LANES - 1):
-            nc.vector.tensor_copy(gathered[:, t, :], planes[t][:].indirect(offsets[:]))
+        for r in range(LANES):
+            nc.vector.tensor_copy(gathered[:, r, :], planes[r][:].indirect(offsets[:]))
 
-        wd_codes, x_codes, x_scale = [], [], []
-        for h in range(2):
-            cols = slice(h * HALF, (h + 1) * HALF)
-            nc.vector.tensor_copy(gathered[:, LANES - 1, cols], planes[LANES - 1][:].indirect(listed(h)))
-            woven = keep.tile([P, HALF, LANES], BF16, name=f"woven{h}", tag=f"woven{h}", align_bytes=64)
+        wd_scale, wd_codes, x_codes, x_scale = [], [], [], []
+        for s in range(2):
+            dealt = keep.tile([P, 3 * PASS], U8, name=f"dealt{s}", tag=("dealt0", "woven0")[s], align_bytes=64)
+            wd_codes.append(dealt[:, : 2 * PASS])
+            wd_scale.append(dealt[:, 2 * PASS :])
             nc.vector.tensor_copy(
-                woven[:].rearrange("p (c i) t -> p c t i", i=4),
-                gathered[:, :, cols].rearrange("p t (c i) -> p c t i", i=4),
+                wd_scale[s].rearrange("p (r c) -> p r c", r=LANES),
+                wd_scale_raw[:, s * PASS : (s + 1) * PASS].rearrange("p (c r) -> p r c", r=LANES),
             )
-            dealt = keep.tile([P, 2 * PASS], U8, name=f"wd_codes{h}", align_bytes=64)
+            woven = keep.tile([P, HALF, LANES], BF16, name=f"woven{s}", tag=("woven0", "second_half_gate")[s], align_bytes=64)
+            (nc.vector.tensor_copy, nc.scalar.copy)[s](
+                woven[:].rearrange("p (c i) r -> p c r i", i=4),
+                gathered[:, :, s * HALF : (s + 1) * HALF].rearrange("p r (c i) -> p c r i", i=4),
+            )
             nc.vector.tensor_copy(
-                dealt[:].bitcast(U16).rearrange("p (r s) -> p r s", r=LANES),
-                wd_raw[:].bitcast(U16)[:, h * PASS : (h + 1) * PASS].rearrange("p (s r) -> p r s", r=LANES),
+                wd_codes[s].bitcast(U16).rearrange("p (r c) -> p r c", r=LANES),
+                wd_raw[:].bitcast(U16)[:, s * PASS : (s + 1) * PASS].rearrange("p (c r) -> p r c", r=LANES),
             )
-            wd_codes.append(dealt)
-            codes = keep.tile([P, HALF], U32, name=f"x_codes{h}", align_bytes=64)
-            scale = keep.tile([P, HALF], U8, name=f"x_scale{h}", align_bytes=64)
-            nc.vector.quantize_mx(codes[:].bitcast(E4M3), scale[:], woven[:].rearrange("p i t -> p (i t)"))
-            x_codes.append(codes)
-            x_scale.append(scale)
+            x_codes.append(keep.tile([P, HALF], U32, name=f"x_codes{s}", align_bytes=64))
+            x_scale.append(keep.tile([P, HALF], U8, name=f"x_scale{s}", align_bytes=64))
+            nc.vector.quantize_mx(x_codes[s][:].bitcast(E4M3), x_scale[s][:], woven[:].rearrange("p i r -> p (i r)"))
 
-        sig, weighted, g_in, dx = {}, {}, {}, {}
+        sig, margin, weighted, g_in = {}, {}, {}, {}
+
+        def open_half(h, tag):
+            work = keep.tile([P, 2, PASSES, LANES, HALF], F32, name=f"work{h}", tag=tag, align_bytes=64)
+            for o in range(PASSES):
+                margin[o, h] = work[:, 0, o, :, :]
+                weighted[o, h] = work[:, 1, o, :, :]
 
         def scores(o, h):
             sig[o, h] = ring.tile([P, LANES, HALF], F32, name="sig")
-            for pair in range(2):
-                bank = score_psum.tile([P, 2, HALF], F32, name="bank")
-                for e in range(2):
-                    r = 2 * pair + e
+            for first in range(0, LANES, PAIR):
+                lanes = slice(first, first + PAIR)
+                bank = psum.tile([P, PAIR, HALF], F32, name="bank", tag=f"bank{(o * LANES + first) // PAIR}")
+                for r in range(first, first + PAIR):
                     nc.tensor.matmul_mx(
-                        bank[:, e, :],
+                        bank[:, r - first, :],
                         lhsT=wd_codes[o][:, 2 * P * r : 2 * P * (r + 1)].bitcast(E2M1),
-                        lhsT_scale=wd_scale[:, o * PASS + P * r : o * PASS + P * (r + 1)],
+                        lhsT_scale=wd_scale[o][:, P * r : P * (r + 1)],
                         rhs=x_codes[h][:].bitcast(E4M3),
                         rhs_scale=x_scale[h][:],
                         start=True,
                         stop=True,
                     )
-                margin = ring.tile([P, 2, HALF], F32, name="margin", bufs=4)
-                nc.vector.tensor_tensor(margin[:], bank[:], labels[o, h][:, 2 * pair : 2 * pair + 2, :], MULT)
-                nc.scalar.activation(sig[o, h][:, 2 * pair : 2 * pair + 2, :], margin[:], SIGMOID, scale=-1.0)
+                nc.vector.tensor_tensor(margin[o, h][:, lanes, :], bank[:], labels[o, h][:, lanes, :], MULT)
+                nc.scalar.activation(sig[o, h][:, lanes, :], margin[o, h][:, lanes, :], SIGMOID, scale=-1.0)
 
-        def weigh(o, h, engine, tag):
-            weighted[o, h] = keep.tile([P, LANES, HALF], F32, name=f"weighted{o}{h}", tag=tag, align_bytes=64)
-            engine.tensor_tensor(weighted[o, h][:], labels[o, h][:], factor[o][:, :, h * HALF : (h + 1) * HALF], MULT)
+        def weigh(h):
+            for first in range(0, LANES, PAIR):
+                lanes = slice(first, first + PAIR)
+                nc.gpsimd.tensor_tensor(
+                    weighted[0, h][:, lanes, :], labels[0, h][:, lanes, :], factor[:, lanes, h * HALF : (h + 1) * HALF], MULT
+                )
+            for r in range(LANES):
+                nc.vector.scalar_tensor_tensor(
+                    weighted[1, h][:, r, :].rearrange("p (k j) -> p k j", j=LANES),
+                    labels[1, h][:, r, :].rearrange("p (k j) -> p k j", j=LANES),
+                    neg_cw[1][:, r : r + 1],
+                    rw_row[:, h * HALF // LANES : (h + 1) * HALF // LANES, :],
+                    MULT,
+                    MULT,
+                )
 
-        def gradient(o, h, first, count):
-            if first == 0:
-                g_in[o, h] = keep.tile([P, HALF, LANES], BF16, name=f"g_in{o}{h}", tag=f"g_in{o}{h}", align_bytes=64)
-            cols = slice(first, first + count)
+        def gradient(o, h):
+            g_in[o, h] = keep.tile([P, HALF, LANES], BF16, name=f"g_in{o}{h}", tag=f"g_in{o}{h}", align_bytes=64)
             nc.vector.tensor_tensor(
-                g_in[o, h][:, cols, :].rearrange("p (c i) t -> p c t i", i=2),
-                sig[o, h][:, :, cols].rearrange("p t (c i) -> p c t i", i=2),
-                weighted[o, h][:, :, cols].rearrange("p t (c i) -> p c t i", i=2),
+                g_in[o, h][:].rearrange("p (c i) r -> p c r i", i=2),
+                sig[o, h][:].rearrange("p r (c i) -> p c r i", i=2),
+                weighted[o, h].rearrange("p r (c i) -> p c r i", i=2),
                 MULT,
             )
 
-        def quantise(o, h, first, count):
-            cols = slice(h * HALF + first, h * HALF + first + count)
+        def quantise(o, h):
+            cols = slice(h * HALF, (h + 1) * HALF)
             nc.vector.quantize_mx(
-                g_codes[o][:, cols].bitcast(E5M2),
-                g_scale[o][:, cols],
-                g_in[o, h][:, first : first + count, :].rearrange("p i t -> p (i t)"),
+                g_codes[o][:, cols].bitcast(E5M2), g_scale[o][:, cols], g_in[o, h][:].rearrange("p i r -> p (i r)")
             )
 
-        def back(bank, o, j):
-            nc.tensor.matmul_mx(
-                bank[:],
-                lhsT=wv_codes[:, o, 2 * P * j : 2 * P * (j + 1)].bitcast(E2M1),
-                lhsT_scale=wv_scale[:, o, P * j : P * (j + 1)],
-                rhs=g_codes[o][:].bitcast(E5M2),
-                rhs_scale=g_scale[o][:],
-                start=(o == 0),
-                stop=(o == PASSES - 1),
-            )
-
-        scores(0, 0)
-        weigh(0, 0, nc.vector, "w00")
-        scores(1, 0)
-        gradient(0, 0, 0, HALF)
-        weigh(1, 0, nc.vector, "w10")
-        quantise(0, 0, 0, HALF)
-        gradient(1, 0, 0, HALF)
-        scores(0, 1)
-        quantise(1, 0, 0, HALF)
-        for j in range(EARLY):
-            bank = grad_psum.tile([P, N], F32, name=f"grad{j}")
+        def back(bank, j):
             for o in range(PASSES):
-                back(bank, o, j)
-            dx[j, 0] = keep.tile([P, HALF], F32, name=f"dx_early{j}")
-            nc.scalar.copy(dx[j, 0][:], bank[:, :HALF])
-        weigh(0, 1, nc.vector, "w01")
-        scores(1, 1)
-        gradient(0, 1, 0, HALF)
-        weigh(1, 1, nc.vector, "w11")
-        quantise(0, 1, 0, HALF)
-        grad = [grad_psum.tile([P, N], F32, name=f"grad{j}") for j in range(D // P)]
-        for j in range(D // P):
-            back(grad[j], 0, j)
-        gradient(1, 1, 0, HALF // 2)
-        gradient(1, 1, HALF // 2, HALF // 2)
-        quantise(1, 1, 0, HALF // 2)
-        quantise(1, 1, HALF // 2, HALF // 2)
-        for j in range(D // P):
-            back(grad[j], 1, j)
-        for j in range(EARLY):
-            nc.vector.tensor_copy(windows[j][:].indirect(listed(0)), dx[j, 0][:])
-        for j in range(D // P):
-            if j < EARLY:
-                dx[j, 1] = keep.tile([P, HALF], F32, name=f"dx{j}")
-                nc.scalar.copy(dx[j, 1][:], grad[j][:, HALF:])
-                nc.vector.tensor_copy(windows[j][:].indirect(listed(1)), dx[j, 1][:])
+                nc.tensor.matmul_mx(
+                    bank[:],
+                    lhsT=wv_codes[:, o, 2 * P * j : 2 * P * (j + 1)].bitcast(E2M1),
+                    lhsT_scale=wv_scale[:, o, P * j : P * (j + 1)],
+                    rhs=g_codes[o][:].bitcast(E5M2),
+                    rhs_scale=g_scale[o][:],
+                    start=(o == 0),
+                    stop=(o == PASSES - 1),
+                )
+
+        def scatter(j, source, entries, tag):
+            dx = keep.tile(list(source.shape), F32, name=f"dx{j}", tag=tag, align_bytes=64)
+            nc.scalar.copy(dx[:], source)
+            nc.vector.tensor_copy(windows[j][:].indirect(entries), dx[:])
+
+        def half(h, tag):
+            open_half(h, tag)
+            for o in range(PASSES):
+                scores(o, h)
+            weigh(h)
+            for o in range(PASSES):
+                gradient(o, h)
+            for o in range(PASSES):
+                quantise(o, h)
+
+        half(0, "second_half_gate")
+        early = psum.tile([P, N], F32, name="early")
+        back(early, 0)
+        half(1, "g_in10")
+
+        scatter(0, early[:, :HALF], listed(0), "g_in10")
+        for j in range(OUT_TILES):
+            grad = psum.tile([P, N], F32, name=f"grad{j}", tag=f"bank{j}")
+            back(grad, j)
+            if j == 0:
+                scatter(j, grad[:, HALF:], listed(1), f"dx{j}")
             else:
-                dx[j, 1] = keep.tile([P, N], F32, name=f"dx{j}")
-                nc.scalar.copy(dx[j, 1][:], grad[j][:])
-                nc.vector.tensor_copy(windows[j][:].indirect(offsets[:]), dx[j, 1][:])
+                scatter(j, grad[:], offsets[:], f"dx{j}")
             nc.sync.dma_start(out[P * j : P * (j + 1), :], windows[j][:])

@@ -27,6 +27,8 @@ HALF = N // 2
 QUADRANTS = 4
 OUT_TILES = D // P
 PAIR = 2
+TILES = PASSES * LANES
+GPSIMD_TILES = 5
 
 
 def tile_attend_gml_sig_kernel(tc, xT, wd_words, wd_scales, wv_words, wv_scales, y, cw, rw, offs, out):
@@ -49,7 +51,6 @@ def tile_attend_gml_sig_kernel(tc, xT, wd_words, wd_scales, wv_words, wv_scales,
         nc.vector.memset(wv_scale[:].rearrange("p o d -> p (o d)").bitcast(I32), 0)
 
         rw_cols = keep.tile([P, LANES], F32, name="rw_cols")
-        nc.sync.dma_start(rw_cols[:], rw[0:1, :].rearrange("one (p j) -> (one p) j", j=LANES))
         cw_cols = keep.tile([P, PASSES, LANES], F32, name="cw_cols")
         nc.scalar.dma_start(cw_cols[:], cw.rearrange("(o p r) one -> p o (r one)", o=PASSES, r=LANES))
 
@@ -57,6 +58,7 @@ def tile_attend_gml_sig_kernel(tc, xT, wd_words, wd_scales, wv_words, wv_scales,
         planes = [keep.tile([P, T], F32, name=f"plane{r}") for r in range(LANES)]
         nc.sync.dma_start(planes[0][:], x_rows[0])
         nc.sync.dma_start(offsets[:], offs)
+        nc.sync.dma_start(rw_cols[:], rw[0:1, :].rearrange("one (p j) -> (one p) j", j=LANES))
         for r in range(1, LANES):
             nc.sync.dma_start(planes[r][:], x_rows[r])
         for q in range(QUADRANTS):
@@ -100,20 +102,21 @@ def tile_attend_gml_sig_kernel(tc, xT, wd_words, wd_scales, wv_words, wv_scales,
             (nc.vector if j < OUT_TILES // 2 else nc.gpsimd).memset(window[:].bitcast(I32), 0)
             windows.append(window)
 
-        neg_cw = []
-        for o, tag in enumerate(("second_half_gate", "neg_cw1")):
-            neg_cw.append(keep.tile([P, LANES], F32, name=f"neg_cw{o}", tag=tag, align_bytes=64))
-            nc.scalar.mul(neg_cw[o][:], cw_cols[:, o, :], -1.0)
+        cw_tiles = cw_cols[:].rearrange("p o r -> p (o r)")
+        neg_cw_gpsimd = keep.tile([P, GPSIMD_TILES], F32, name="neg_cw_gpsimd", tag="first_half_gate", align_bytes=64)
+        neg_cw_vector = keep.tile([P, TILES - GPSIMD_TILES], F32, name="neg_cw_vector")
+        nc.scalar.mul(neg_cw_gpsimd[:], cw_tiles[:, :GPSIMD_TILES], -1.0)
+        nc.scalar.mul(neg_cw_vector[:], cw_tiles[:, GPSIMD_TILES:], -1.0)
 
         rw_bank = psum.tile([P, LANES, P], F32, name="rw_bank")
         for j in range(LANES):
             nc.tensor.transpose(rw_bank[:, j, :], rw_cols[:, j : j + 1].to_broadcast([P, P]), identity[:])
-        rw_row = rw_bank[:].rearrange("p j k -> p k j")
+        rw_row = rw_bank[:].rearrange("p j c -> p c j")
 
-        factor = keep.tile([P, LANES, N], F32, name="factor")
-        for r in range(LANES):
+        factor = keep.tile([P, GPSIMD_TILES, N], F32, name="factor")
+        for k in range(GPSIMD_TILES):
             nc.scalar.activation(
-                factor[:, r, :].rearrange("p (k j) -> p k j", j=LANES), rw_row, COPY, scale=neg_cw[0][:, r : r + 1]
+                factor[:, k, :].rearrange("p (c j) -> p c j", j=LANES), rw_row, COPY, scale=neg_cw_gpsimd[:, k : k + 1]
             )
 
         gathered = keep.tile([P, LANES, N], BF16, name="gathered")
@@ -129,7 +132,7 @@ def tile_attend_gml_sig_kernel(tc, xT, wd_words, wd_scales, wv_words, wv_scales,
                 wd_scale[s].rearrange("p (r c) -> p r c", r=LANES),
                 wd_scale_raw[:, s * PASS : (s + 1) * PASS].rearrange("p (c r) -> p r c", r=LANES),
             )
-            woven = keep.tile([P, HALF, LANES], BF16, name=f"woven{s}", tag=("woven0", "second_half_gate")[s], align_bytes=64)
+            woven = keep.tile([P, HALF, LANES], BF16, name=f"woven{s}", tag=("woven0", "first_half_gate")[s], align_bytes=64)
             (nc.vector.tensor_copy, nc.scalar.copy)[s](
                 woven[:].rearrange("p (c i) r -> p c r i", i=4),
                 gathered[:, :, s * HALF : (s + 1) * HALF].rearrange("p r (c i) -> p c r i", i=4),
@@ -169,16 +172,19 @@ def tile_attend_gml_sig_kernel(tc, xT, wd_words, wd_scales, wv_words, wv_scales,
                 nc.scalar.activation(sig[o, h][:, lanes, :], margin[o, h][:, lanes, :], SIGMOID, scale=-1.0)
 
         def weigh(h):
-            for first in range(0, LANES, PAIR):
-                lanes = slice(first, first + PAIR)
+            for first in range(0, GPSIMD_TILES, PAIR):
+                last = min(first + PAIR, GPSIMD_TILES)
+                o = first // LANES
+                lanes = slice(first - o * LANES, last - o * LANES)
                 nc.gpsimd.tensor_tensor(
-                    weighted[0, h][:, lanes, :], labels[0, h][:, lanes, :], factor[:, lanes, h * HALF : (h + 1) * HALF], MULT
+                    weighted[o, h][:, lanes, :], labels[o, h][:, lanes, :], factor[:, first:last, h * HALF : (h + 1) * HALF], MULT
                 )
-            for r in range(LANES):
+            for k in range(GPSIMD_TILES, TILES):
+                o, r = divmod(k, LANES)
                 nc.vector.scalar_tensor_tensor(
-                    weighted[1, h][:, r, :].rearrange("p (k j) -> p k j", j=LANES),
-                    labels[1, h][:, r, :].rearrange("p (k j) -> p k j", j=LANES),
-                    neg_cw[1][:, r : r + 1],
+                    weighted[o, h][:, r, :].rearrange("p (c j) -> p c j", j=LANES),
+                    labels[o, h][:, r, :].rearrange("p (c j) -> p c j", j=LANES),
+                    neg_cw_vector[:, k - GPSIMD_TILES : k - GPSIMD_TILES + 1],
                     rw_row[:, h * HALF // LANES : (h + 1) * HALF // LANES, :],
                     MULT,
                     MULT,
@@ -226,14 +232,14 @@ def tile_attend_gml_sig_kernel(tc, xT, wd_words, wd_scales, wv_words, wv_scales,
             for o in range(PASSES):
                 quantise(o, h)
 
-        half(0, "second_half_gate")
+        half(0, "first_half_gate")
         early = psum.tile([P, N], F32, name="early")
         back(early, 0)
         half(1, "g_in10")
 
         scatter(0, early[:, :HALF], listed(0), "g_in10")
-        for j in range(OUT_TILES):
-            grad = psum.tile([P, N], F32, name=f"grad{j}", tag=f"bank{j}")
+        for j in (1, 0, *range(2, OUT_TILES)):
+            grad = psum.tile([P, N], F32, name="grad")
             back(grad, j)
             if j == 0:
                 scatter(j, grad[:, HALF:], listed(1), f"dx{j}")

from contextlib import ExitStack

import concourse.mybir as mybir
from concourse.masks import make_identity

N, T, D, V = 512, 1024, 512, 1024
FLOPS = 2 * 2 * N * D * V

F32 = mybir.dt.float32
BF16 = mybir.dt.bfloat16
I32 = mybir.dt.int32
U32 = mybir.dt.uint32
U16 = mybir.dt.uint16
U8 = mybir.dt.uint8
E4M3 = mybir.dt.float8_e4m3fn_x4
E5M2 = mybir.dt.float8_e5m2_x4
E2M1 = mybir.dt.float4_e2m1fn_x4
MULT = mybir.AluOpType.mult
SIGMOID = mybir.ActivationFunctionType.Sigmoid
COPY = mybir.ActivationFunctionType.Copy

P = 128
LANES = 4
PASS = P * LANES
PASSES = V // PASS
HALF = N // 2
QUADRANTS = 4
OUT_TILES = D // P
PAIR = 2
TILES = PASSES * LANES
GPSIMD_TILES = 5


def tile_attend_gml_sig_kernel(tc, xT, wd_words, wd_scales, wv_words, wv_scales, y, cw, rw, offs, out):
    nc = tc.nc
    with ExitStack() as ctx:
        keep = ctx.enter_context(tc.tile_pool(name="keep", bufs=1))
        ring = ctx.enter_context(tc.tile_pool(name="ring", bufs=2))
        psum = ctx.enter_context(tc.psum_pool(name="psum", bufs=1))

        offsets = keep.tile([P, N // 16], U16, name="offsets")

        def listed(h):
            return offsets[:, h * HALF // 16 : (h + 1) * HALF // 16]

        wd_scale_raw = keep.tile([P, V], U8, name="wd_scale_raw", align_bytes=64)
        wv_scale = keep.tile([P, PASSES, D], U8, name="wv_scale", align_bytes=64)
        nc.gpsimd.memset(wd_scale_raw[:].bitcast(I32), 0)
        identity = keep.tile([P, P], F32, name="identity")
        make_identity(nc, identity[:])
        nc.vector.memset(wv_scale[:].rearrange("p o d -> p (o d)").bitcast(I32), 0)

        rw_cols = keep.tile([P, LANES], F32, name="rw_cols")
        cw_cols = keep.tile([P, PASSES, LANES], F32, name="cw_cols")
        nc.scalar.dma_start(cw_cols[:], cw.rearrange("(o p r) one -> p o (r one)", o=PASSES, r=LANES))

        x_rows = xT.rearrange("(p r) n -> r p n", r=LANES)
        planes = [keep.tile([P, T], F32, name=f"plane{r}") for r in range(LANES)]
        nc.sync.dma_start(planes[0][:], x_rows[0])
        nc.sync.dma_start(offsets[:], offs)
        nc.sync.dma_start(rw_cols[:], rw[0:1, :].rearrange("one (p j) -> (one p) j", j=LANES))
        for r in range(1, LANES):
            nc.sync.dma_start(planes[r][:], x_rows[r])
        for q in range(QUADRANTS):
            nc.sync.dma_start(
                wd_scale_raw[32 * q : 32 * q + 4, :].bitcast(I32),
                wd_scales[0, 4 * q : 4 * q + 4, :].bitcast(I32),
            )
        wd_raw = keep.tile([P, 2 * V], U8, name="wd_raw", align_bytes=64)
        nc.sync.dma_start(wd_raw[:].bitcast(I32), wd_words[0].bitcast(I32))

        y_rows = y.rearrange("(o p r) n -> o p r n", o=PASSES, r=LANES)
        labels = {}

        def load_labels(h):
            for o in range(PASSES):
                labels[o, h] = keep.tile([P, LANES, HALF], F32, name=f"labels{o}{h}")
                nc.sync.dma_start(labels[o, h][:], y_rows[o, :, :, h * HALF : (h + 1) * HALF])

        load_labels(0)
        wv_codes = keep.tile([P, PASSES, 2 * D], U8, name="wv_codes", align_bytes=64)
        nc.sync.dma_start(
            wv_codes[:].rearrange("p o n -> p (o n)").bitcast(I32).rearrange("p (o n) -> p o n", o=PASSES),
            wv_words.bitcast(I32).rearrange("o p n -> p o n"),
        )
        load_labels(1)
        for q in range(QUADRANTS):
            nc.sync.dma_start(
                wv_scale[32 * q : 32 * q + 4, :, :].rearrange("p o d -> p (o d)").bitcast(I32).rearrange("p (o d) -> p o d", o=PASSES),
                wv_scales.bitcast(I32)[:, 4 * q : 4 * q + 4, :].rearrange("o f d -> f o d"),
            )

        g_codes = [keep.tile([P, N], U32, name=f"g_codes{o}", align_bytes=64) for o in range(PASSES)]
        g_scale = [keep.tile([P, N], U8, name=f"g_scale{o}", align_bytes=64) for o in range(PASSES)]
        for o in range(PASSES):
            nc.vector.memset(g_codes[o][:, HALF:].bitcast(I32), 0)
            nc.vector.memset(g_scale[o][:, HALF:].bitcast(I32), 0)

        windows = []
        for j in range(OUT_TILES):
            window = keep.tile([P, T], F32, name=f"window{j}")
            (nc.vector if j < OUT_TILES // 2 else nc.gpsimd).memset(window[:].bitcast(I32), 0)
            windows.append(window)

        cw_tiles = cw_cols[:].rearrange("p o r -> p (o r)")
        neg_cw_gpsimd = keep.tile([P, GPSIMD_TILES], F32, name="neg_cw_gpsimd", tag="first_half_gate", align_bytes=64)
        neg_cw_vector = keep.tile([P, TILES - GPSIMD_TILES], F32, name="neg_cw_vector")
        nc.scalar.mul(neg_cw_gpsimd[:], cw_tiles[:, :GPSIMD_TILES], -1.0)
        nc.scalar.mul(neg_cw_vector[:], cw_tiles[:, GPSIMD_TILES:], -1.0)

        rw_bank = psum.tile([P, LANES, P], F32, name="rw_bank")
        for j in range(LANES):
            nc.tensor.transpose(rw_bank[:, j, :], rw_cols[:, j : j + 1].to_broadcast([P, P]), identity[:])
        rw_row = rw_bank[:].rearrange("p j c -> p c j")

        factor = keep.tile([P, GPSIMD_TILES, N], F32, name="factor")
        for k in range(GPSIMD_TILES):
            nc.scalar.activation(
                factor[:, k, :].rearrange("p (c j) -> p c j", j=LANES), rw_row, COPY, scale=neg_cw_gpsimd[:, k : k + 1]
            )

        gathered = keep.tile([P, LANES, N], BF16, name="gathered")
        for r in range(LANES):
            nc.vector.tensor_copy(gathered[:, r, :], planes[r][:].indirect(offsets[:]))

        wd_scale, wd_codes, x_codes, x_scale = [], [], [], []
        for s in range(2):
            dealt = keep.tile([P, 3 * PASS], U8, name=f"dealt{s}", tag=("dealt0", "woven0")[s], align_bytes=64)
            wd_codes.append(dealt[:, : 2 * PASS])
            wd_scale.append(dealt[:, 2 * PASS :])
            nc.vector.tensor_copy(
                wd_scale[s].rearrange("p (r c) -> p r c", r=LANES),
                wd_scale_raw[:, s * PASS : (s + 1) * PASS].rearrange("p (c r) -> p r c", r=LANES),
            )
            woven = keep.tile([P, HALF, LANES], BF16, name=f"woven{s}", tag=("woven0", "first_half_gate")[s], align_bytes=64)
            (nc.vector.tensor_copy, nc.scalar.copy)[s](
                woven[:].rearrange("p (c i) r -> p c r i", i=4),
                gathered[:, :, s * HALF : (s + 1) * HALF].rearrange("p r (c i) -> p c r i", i=4),
            )
            nc.vector.tensor_copy(
                wd_codes[s].bitcast(U16).rearrange("p (r c) -> p r c", r=LANES),
                wd_raw[:].bitcast(U16)[:, s * PASS : (s + 1) * PASS].rearrange("p (c r) -> p r c", r=LANES),
            )
            x_codes.append(keep.tile([P, HALF], U32, name=f"x_codes{s}", align_bytes=64))
            x_scale.append(keep.tile([P, HALF], U8, name=f"x_scale{s}", align_bytes=64))
            nc.vector.quantize_mx(x_codes[s][:].bitcast(E4M3), x_scale[s][:], woven[:].rearrange("p i r -> p (i r)"))

        sig, margin, weighted, g_in = {}, {}, {}, {}

        def open_half(h, tag):
            work = keep.tile([P, 2, PASSES, LANES, HALF], F32, name=f"work{h}", tag=tag, align_bytes=64)
            for o in range(PASSES):
                margin[o, h] = work[:, 0, o, :, :]
                weighted[o, h] = work[:, 1, o, :, :]

        def scores(o, h):
            sig[o, h] = ring.tile([P, LANES, HALF], F32, name="sig")
            for first in range(0, LANES, PAIR):
                lanes = slice(first, first + PAIR)
                bank = psum.tile([P, PAIR, HALF], F32, name="bank", tag=f"bank{(o * LANES + first) // PAIR}")
                for r in range(first, first + PAIR):
                    nc.tensor.matmul_mx(
                        bank[:, r - first, :],
                        lhsT=wd_codes[o][:, 2 * P * r : 2 * P * (r + 1)].bitcast(E2M1),
                        lhsT_scale=wd_scale[o][:, P * r : P * (r + 1)],
                        rhs=x_codes[h][:].bitcast(E4M3),
                        rhs_scale=x_scale[h][:],
                        start=True,
                        stop=True,
                    )
                nc.vector.tensor_tensor(margin[o, h][:, lanes, :], bank[:], labels[o, h][:, lanes, :], MULT)
                nc.scalar.activation(sig[o, h][:, lanes, :], margin[o, h][:, lanes, :], SIGMOID, scale=-1.0)

        def weigh(h):
            for first in range(0, GPSIMD_TILES, PAIR):
                last = min(first + PAIR, GPSIMD_TILES)
                o = first // LANES
                lanes = slice(first - o * LANES, last - o * LANES)
                nc.gpsimd.tensor_tensor(
                    weighted[o, h][:, lanes, :], labels[o, h][:, lanes, :], factor[:, first:last, h * HALF : (h + 1) * HALF], MULT
                )
            for k in range(GPSIMD_TILES, TILES):
                o, r = divmod(k, LANES)
                nc.vector.scalar_tensor_tensor(
                    weighted[o, h][:, r, :].rearrange("p (c j) -> p c j", j=LANES),
                    labels[o, h][:, r, :].rearrange("p (c j) -> p c j", j=LANES),
                    neg_cw_vector[:, k - GPSIMD_TILES : k - GPSIMD_TILES + 1],
                    rw_row[:, h * HALF // LANES : (h + 1) * HALF // LANES, :],
                    MULT,
                    MULT,
                )

        def gradient(o, h):
            g_in[o, h] = keep.tile([P, HALF, LANES], BF16, name=f"g_in{o}{h}", tag=f"g_in{o}{h}", align_bytes=64)
            nc.vector.tensor_tensor(
                g_in[o, h][:].rearrange("p (c i) r -> p c r i", i=2),
                sig[o, h][:].rearrange("p r (c i) -> p c r i", i=2),
                weighted[o, h].rearrange("p r (c i) -> p c r i", i=2),
                MULT,
            )

        def quantise(o, h):
            cols = slice(h * HALF, (h + 1) * HALF)
            nc.vector.quantize_mx(
                g_codes[o][:, cols].bitcast(E5M2), g_scale[o][:, cols], g_in[o, h][:].rearrange("p i r -> p (i r)")
            )

        def back(bank, j):
            for o in range(PASSES):
                nc.tensor.matmul_mx(
                    bank[:],
                    lhsT=wv_codes[:, o, 2 * P * j : 2 * P * (j + 1)].bitcast(E2M1),
                    lhsT_scale=wv_scale[:, o, P * j : P * (j + 1)],
                    rhs=g_codes[o][:].bitcast(E5M2),
                    rhs_scale=g_scale[o][:],
                    start=(o == 0),
                    stop=(o == PASSES - 1),
                )

        def scatter(j, source, entries, tag):
            dx = keep.tile(list(source.shape), F32, name=f"dx{j}", tag=tag, align_bytes=64)
            nc.scalar.copy(dx[:], source)
            nc.vector.tensor_copy(windows[j][:].indirect(entries), dx[:])

        def half(h, tag):
            open_half(h, tag)
            for o in range(PASSES):
                scores(o, h)
            weigh(h)
            for o in range(PASSES):
                gradient(o, h)
            for o in range(PASSES):
                quantise(o, h)

        half(0, "first_half_gate")
        early = psum.tile([P, N], F32, name="early")
        back(early, 0)
        half(1, "g_in10")

        scatter(0, early[:, :HALF], listed(0), "g_in10")
        for j in (1, 0, *range(2, OUT_TILES)):
            grad = psum.tile([P, N], F32, name="grad")
            back(grad, j)
            if j == 0:
                scatter(j, grad[:, HALF:], listed(1), f"dx{j}")
            else:
                scatter(j, grad[:], offsets[:], f"dx{j}")
            nc.sync.dma_start(out[P * j : P * (j + 1), :], windows[j][:])
